import numpy as np
import ml_dtypes


def mxq(x, axis, fmt="e4m3"):
    dtype, down = {"e4m3": (ml_dtypes.float8_e4m3fn, 7), "e5m2": (ml_dtypes.float8_e5m2, 14)}[fmt]
    v = np.moveaxis(np.asarray(x, np.float32).astype(ml_dtypes.bfloat16).astype(np.float64), axis, -1)
    blocks = v.reshape(v.shape[:-1] + (-1, 32))
    amax = np.abs(blocks).max(-1, keepdims=True)
    byte = np.maximum(np.where(amax > 0, np.frexp(amax)[1] - 1 + 127, 0) - down, 1)
    scale = np.exp2(byte - 127.0)
    codes = (blocks / scale).astype(np.float32).astype(dtype).astype(np.float64)
    return np.moveaxis((codes * scale).reshape(v.shape), -1, axis)


WIDE = False


def mx_kscale(k):
    if not WIDE:
        return np.ones(k)
    levels = np.array([10, -10, 5, -5, 0])
    if k % 512:
        return np.exp2(np.random.permutation(np.resize(levels, k // 32))).repeat(32)
    a = np.empty((k // 512, 16))
    for p in range(k // 512):
        a[p, :8] = np.random.permutation(np.resize(levels, 8))
        for g in range(8):
            far = levels[np.abs(levels - a[p, g]) >= 10]
            a[p, g + 8] = far[np.random.randint(len(far))]
    return np.exp2(a.ravel()).repeat(32)


def f64(x):
    return np.asarray(x).astype(np.float64)


def striped(idx):
    return np.tile(idx.reshape(-1, 16).T, (8, 1)).astype(np.uint16)


def unstriped(offs):
    return offs[:16].T.reshape(-1).astype(np.int64)


def pack_weight(w):
    k, n = w.shape
    w = f64(np.asarray(w, np.float32).astype(ml_dtypes.bfloat16)).reshape(k // 32, 32, n)
    amax = np.abs(w).max(1)
    byte = np.clip(np.where(amax > 0, np.frexp(amax)[1] - 1 + 127 - 7, 1), 1, 254)
    scaled = (w * np.exp2(127.0 - byte)[:, None, :]).reshape(k, n).astype(np.float32)
    words = np.ascontiguousarray(scaled.reshape(k // 512, 128, 4, n).transpose(0, 1, 3, 2)).astype(ml_dtypes.float8_e4m3fn).view(np.uint8)
    return words, np.ascontiguousarray(byte.astype(np.uint8).reshape(k // 512, 16, n))


def unpack_weight(words, scales):
    g, p, n, _ = words.shape
    vals = np.ascontiguousarray(words).view(ml_dtypes.float8_e4m3fn).astype(np.float64) * np.repeat(np.exp2(scales.astype(np.float64) - 127.0), 8, axis=1)[..., None]
    return vals.transpose(0, 1, 3, 2).reshape(g * 512, n)


def planes(y):
    n, m = y.shape
    v = y.astype(np.float32).astype(ml_dtypes.bfloat16).astype(np.float64).reshape(n // 32, 32, m)
    top = np.abs(v).max(1)
    byte = np.clip(np.where(top > 0, np.frexp(top)[1] - 1 + 127 - 7, 1), 1, 254)
    codes = (v * np.exp2(127.0 - byte)[:, None, :]).reshape(n, m).astype(np.float32).astype(ml_dtypes.float8_e4m3fn).view(np.uint8)
    words = codes.reshape(n // 512, 128, 4, m).transpose(0, 1, 3, 2)
    return np.ascontiguousarray(words), np.ascontiguousarray(byte.astype(np.uint8).reshape(n // 512, 16, m))


def relu(v):
    return np.maximum(v, 0.0)


K, T, S, D, V, H, N = 512, 2048, 1024, 2, 512, 512, 512


def setup_inputs():
    n = np.random.standard_normal
    s = mx_kscale(K)[:, None]
    u = mx_kscale(H)
    packed_xT = pack_weight(n((K, T)) * s)
    return {
        "x_words": packed_xT[0],
        "x_scales": packed_xT[1],
        "w1": (n((K, H)) / np.sqrt(K) / s * u).astype(np.float32),
        "w2": (n((K, N)) / np.sqrt(K) / s).astype(np.float32),
        "w3": (n((H, N)) / np.sqrt(H) / u[:, None]).astype(np.float32),
        "offs": striped(np.random.permutation(T)[:S]),
    }


def reference(x_words, x_scales, w1, w2, w3, offs):
    xq = unpack_weight(x_words, x_scales)[:, unstriped(offs)]
    h = mxq(f64(w1), 0, "e4m3").T @ xq
    sh = h.reshape(H, V, D).sum(axis=2)
    e = mxq(f64(w2), 0, "e4m3").T @ xq
    se = e.reshape(H, V, D).sum(axis=2)
    z = sh * se - ((h * e).reshape(H, V, D).sum(axis=2))
    out_0 = relu(mxq(f64(w3), 0, "e4m3").T @ mxq(z, 0, "e4m3"))
    return (out_0,) + planes(out_0)

@@ -1,0 +1,145 @@
+from contextlib import ExitStack
+
+import concourse.mybir as mybir
+
+F32 = mybir.dt.float32
+BF16 = mybir.dt.bfloat16
+I32 = mybir.dt.int32
+U32 = mybir.dt.uint32
+U16 = mybir.dt.uint16
+U8 = mybir.dt.uint8
+FP8X4 = mybir.dt.float8_e4m3fn_x4
+ACT = mybir.ActivationFunctionType
+ALU = mybir.AluOpType
+
+P = 128
+K, T, S, V, H, N = 512, 2048, 1024, 512, 512, 512
+FLOPS = 2 * K * H * S * 2 + 2 * H * N * V
+UNITS = 8
+QUARTERS = 4
+GATHER = 256
+
+
+def tile_picked_zfm_relu_po_kernel(tc, x_words, x_scales, w1, w2, w3, offs, out_0, out_1, out_2):
+    nc = tc.nc
+    with ExitStack() as ctx:
+        keep = ctx.enter_context(tc.tile_pool(name="keep", bufs=1))
+        ring = ctx.enter_context(tc.tile_pool(name="ring", bufs=3))
+        psum = ctx.enter_context(tc.psum_pool(name="psum", bufs=1))
+
+        offsets = keep.tile([P, S // 16], U16, name="offsets")
+        table_words = keep.tile([P, T], U32, name="table_words", align_bytes=64)
+        table_scales = keep.tile([P, T], U8, name="table_scales", align_bytes=64)
+        raw1 = keep.tile([P, 4, H], F32, name="raw1", tag="raw13", align_bytes=64)
+        raw2 = keep.tile([P, 4, H], F32, name="raw2", tag="raw2", align_bytes=64)
+
+        nc.vector.memset(table_scales[:].bitcast(I32), 0)
+        nc.sync.dma_start(out=offsets[:], in_=offs)
+        words_in = x_words[0].rearrange("p c r -> p (c r)").bitcast(I32)
+        nc.sync.dma_start(out=table_words[:, 0:512].bitcast(I32), in_=words_in[:, 0:512])
+        for q in range(4):
+            nc.sync.dma_start(out=table_scales[32 * q : 32 * q + 4, :].bitcast(I32), in_=x_scales[0, 4 * q : 4 * q + 4, :].bitcast(I32))
+        nc.sync.dma_start(out=raw1[:], in_=w1.rearrange("(p j) c -> p j c", j=4))
+        nc.sync.dma_start(out=table_words[:, 512:T].bitcast(I32), in_=words_in[:, 512:T])
+        nc.sync.dma_start(out=raw2[:], in_=w2.rearrange("(p j) c -> p j c", j=4))
+
+        x_scale = keep.tile([P, S], U8, name="x_scale", align_bytes=64)
+        nc.vector.tensor_copy(out=x_scale[:], in_=table_scales[:].indirect(offsets[:]))
+
+        def round_slot(raw, t, on_scalar, tag):
+            grouped = keep.tile([P, P * 4], BF16, name=f"{tag}_grouped{t}", tag=f"{tag}_slot{t}", align_bytes=64)
+            src = raw[:].rearrange("p j (s t b) -> p t s b j", t=4, b=4)[:, t]
+            dst = grouped[:].rearrange("p (s b j) -> p s b j", b=4, j=4)
+            if on_scalar:
+                nc.scalar.activation(out=dst, in_=src, func=ACT.Copy)
+            else:
+                nc.vector.tensor_copy(out=dst, in_=src)
+            return grouped
+
+        def quantize(grouped, tag):
+            width = grouped.shape[1] // 4
+            codes = keep.tile([P, width], U32, name=f"{tag}_codes", align_bytes=64)
+            scales = keep.tile([P, width], U8, name=f"{tag}_scales", align_bytes=64)
+            nc.vector.quantize_mx(out=codes[:].bitcast(FP8X4), scales=scales[:], in_=grouped[:])
+            return codes, scales
+
+        g1 = [round_slot(raw1, t, t >= 2, "w1") for t in range(4)]
+        q1 = [quantize(g1[t], f"w1_{t}") for t in range(4)]
+
+        raw3 = keep.tile([P, 4, N], F32, name="raw3", tag="raw13", align_bytes=64)
+        w3_rows = w3.rearrange("(s j b) c -> b s j c", j=4, b=4)
+        for b in range(4):
+            nc.sync.dma_start(out=raw3[b:P:4, :, :], in_=w3_rows[b])
+
+        x_code = []
+        for g in range(S // GATHER):
+            picked = keep.tile([P, GATHER], U32, name=f"x_code{g}", tag=f"w1_slot{g}", align_bytes=64)
+            nc.vector.tensor_copy(out=picked[:], in_=table_words[:].indirect(offsets[:, g * GATHER // 16 : (g + 1) * GATHER // 16]))
+            x_code.append(picked)
+
+        def project(quantized, u, label):
+            bank = psum.tile([P, 4, P], F32, name=f"{label}{u}", tag=f"bank{u}")
+            words = x_code[u // 2][:, (u % 2) * P : (u % 2 + 1) * P]
+            cols = slice(u * P, (u + 1) * P)
+            for t in range(4):
+                nc.tensor.matmul_mx(out=bank[:, t, :], lhsT=quantized[t][0][:].bitcast(FP8X4), lhsT_scale=quantized[t][1][:],
+                                    rhs=words.bitcast(FP8X4), rhs_scale=x_scale[:, cols], start=True, stop=True)
+            return bank
+
+        g3 = keep.tile([P, N * 4], BF16, name="w3_grouped", tag="staged", align_bytes=64)
+        def copy_h(u, h_u):
+            bank = project(q1, u, "h_bank")
+            nc.scalar.copy(out=h_u, in_=bank[:].rearrange("p t (v d) -> p d v t", d=2))
+            return h_u
+
+        h_first = keep.tile([P, 2, 64, 4], F32, name="h_first", align_bytes=64)
+        h_sb = [copy_h(0, h_first[:])]
+        g2 = [round_slot(raw2, t, t >= 2, "w2") for t in range(4)]
+        q2 = [quantize(g2[t], f"w2_{t}") for t in range(4)]
+        h_mid = keep.tile([P, 4, 2, 64, 4], F32, name="h_mid", tag="raw2", align_bytes=64)
+        h_sb.extend(copy_h(u, h_mid[:, u - 1]) for u in range(1, 5))
+        nc.scalar.copy(out=g3[:].rearrange("p (t m j) -> p m t j", t=4, j=4), in_=raw3[:].rearrange("p j (m t) -> p m t j", t=4))
+        h_last = keep.tile([P, 3, 2, 64, 4], F32, name="h_last", tag="raw13", align_bytes=64)
+        h_sb.extend(copy_h(u, h_last[:, u - 5]) for u in range(5, UNITS))
+
+        y_words = keep.tile([P, V], U32, name="y_words", align_bytes=64)
+        y_scales = keep.tile([P, V], U8, name="y_scales", align_bytes=64)
+        out_rows = out_0.rearrange("(p t) v -> p t v", t=4)
+        out_words = out_1[0].rearrange("p c r -> p (c r)").bitcast(I32)
+
+        zq = []
+        for q in range(QUARTERS):
+            if q == 1:
+                w3_codes, w3_scales = quantize(g3, "w3")
+            z = keep.tile([P, 512], BF16, name=f"z{q}", tag="staged" if q == 2 else f"z{q}", align_bytes=64)
+            for a in range(2):
+                u = 2 * q + a
+                prod = ring.tile([P, 2, 256], F32, name="prod", align_bytes=64)
+                bank = project(q2, u, "e_bank")
+                nc.vector.tensor_tensor(out=prod[:].rearrange("p d (v t) -> p d v t", t=4),
+                                        in0=bank[:].rearrange("p t (v d) -> p d v t", d=2),
+                                        in1=h_sb[u][:, ::-1], op=ALU.mult)
+                nc.vector.tensor_tensor(out=z[:, a * 256 : (a + 1) * 256], in0=prod[:, 0, :], in1=prod[:, 1, :], op=ALU.add)
+            zq.append(quantize(z, f"z{q}"))
+
+        for q in range(QUARTERS):
+            cols = slice(q * P, (q + 1) * P)
+            bank = psum.tile([P, 4, P], F32, name=f"y_bank{q}", tag=f"bank{q}")
+            for t in range(4):
+                nc.tensor.matmul_mx(out=bank[:, t, :], lhsT=w3_codes[:, t * P : (t + 1) * P].bitcast(FP8X4), lhsT_scale=w3_scales[:, t * P : (t + 1) * P],
+                                    rhs=zq[q][0][:].bitcast(FP8X4), rhs_scale=zq[q][1][:], start=True, stop=True)
+            y16 = keep.tile([P, 512], BF16, name=f"y16_{q}", align_bytes=64)
+            y32 = keep.tile([P, 4, P], F32, name=f"y32_{q}", align_bytes=64)
+            if q >= 2:
+                nc.scalar.activation(out=y16[:].rearrange("p (v t) -> p v t", t=4), in_=bank[:].rearrange("p t v -> p v t"), func=ACT.Relu)
+            nc.scalar.activation(out=y32[:], in_=bank[:], func=ACT.Relu)
+            if q < 2:
+                nc.vector.tensor_copy(out=y16[:].rearrange("p (v t) -> p v t", t=4), in_=y32[:].rearrange("p t v -> p v t"))
+            nc.vector.quantize_mx(out=y_words[:, cols].bitcast(FP8X4), scales=y_scales[:, cols], in_=y16[:])
+            nc.sync.dma_start(out=out_rows[:, :, cols], in_=y32[:])
+            if q == 2:
+                nc.sync.dma_start(out=out_words[:, 0 : 3 * P], in_=y_words[:, 0 : 3 * P].bitcast(I32))
+        nc.sync.dma_start(out=out_words[:, 3 * P : V], in_=y_words[:, 3 * P : V].bitcast(I32))
+        for q in range(4):
+            queue = nc.sync if q % 2 == 0 else nc.scalar
+            queue.dma_start(out=out_2[0, 4 * q : 4 * q + 4, :].bitcast(I32), in_=y_scales[32 * q : 32 * q + 4, :].bitcast(I32))

@@ -17,116 +17,130 @@ K, T, S, V, H, N = 512, 2048, 1024, 512, 512, 512
 FLOPS = 2 * K * H * S * 2 + 2 * H * N * V
 UNITS = 8
 QUARTERS = 4
-GATHER = 256
+GATHER = 512
 
 
 def tile_picked_zfm_relu_po_kernel(tc, x_words, x_scales, w1, w2, w3, offs, out_0, out_1, out_2):
     nc = tc.nc
     with ExitStack() as ctx:
         keep = ctx.enter_context(tc.tile_pool(name="keep", bufs=1))
-        ring = ctx.enter_context(tc.tile_pool(name="ring", bufs=3))
+        ring = ctx.enter_context(tc.tile_pool(name="ring", bufs=6))
+        reuse = ctx.enter_context(tc.tile_pool(name="reuse", bufs=1))
         psum = ctx.enter_context(tc.psum_pool(name="psum", bufs=1))
 
         offsets = keep.tile([P, S // 16], U16, name="offsets")
         table_words = keep.tile([P, T], U32, name="table_words", align_bytes=64)
         table_scales = keep.tile([P, T], U8, name="table_scales", align_bytes=64)
-        raw1 = keep.tile([P, 4, H], F32, name="raw1", tag="raw13", align_bytes=64)
-        raw2 = keep.tile([P, 4, H], F32, name="raw2", tag="raw2", align_bytes=64)
+        raw1 = keep.tile([P, 4, H], F32, name="raw1", align_bytes=64)
+        raw2_low = reuse.tile([P, 4, H // 2], F32, name="raw2_low", offset=4096)
+        raw2_high = reuse.tile([P, 4, H // 2], F32, name="raw2_high", offset=0)
+        raw3 = reuse.tile([P, 4, N], F32, name="raw3", offset=8192)
 
         nc.vector.memset(table_scales[:].bitcast(I32), 0)
         nc.sync.dma_start(out=offsets[:], in_=offs)
         words_in = x_words[0].rearrange("p c r -> p (c r)").bitcast(I32)
-        nc.sync.dma_start(out=table_words[:, 0:512].bitcast(I32), in_=words_in[:, 0:512])
+        nc.sync.dma_start(out=table_words[:, 0:1024].bitcast(I32), in_=words_in[:, 0:1024])
         for q in range(4):
             nc.sync.dma_start(out=table_scales[32 * q : 32 * q + 4, :].bitcast(I32), in_=x_scales[0, 4 * q : 4 * q + 4, :].bitcast(I32))
+        nc.sync.dma_start(out=table_words[:, 1024:T].bitcast(I32), in_=words_in[:, 1024:T])
         nc.sync.dma_start(out=raw1[:], in_=w1.rearrange("(p j) c -> p j c", j=4))
-        nc.sync.dma_start(out=table_words[:, 512:T].bitcast(I32), in_=words_in[:, 512:T])
-        nc.sync.dma_start(out=raw2[:], in_=w2.rearrange("(p j) c -> p j c", j=4))
-
-        x_scale = keep.tile([P, S], U8, name="x_scale", align_bytes=64)
-        nc.vector.tensor_copy(out=x_scale[:], in_=table_scales[:].indirect(offsets[:]))
-
-        def round_slot(raw, t, on_scalar, tag):
-            grouped = keep.tile([P, P * 4], BF16, name=f"{tag}_grouped{t}", tag=f"{tag}_slot{t}", align_bytes=64)
-            src = raw[:].rearrange("p j (s t b) -> p t s b j", t=4, b=4)[:, t]
-            dst = grouped[:].rearrange("p (s b j) -> p s b j", b=4, j=4)
-            if on_scalar:
-                nc.scalar.activation(out=dst, in_=src, func=ACT.Copy)
-            else:
-                nc.vector.tensor_copy(out=dst, in_=src)
-            return grouped
-
-        def quantize(grouped, tag):
-            width = grouped.shape[1] // 4
-            codes = keep.tile([P, width], U32, name=f"{tag}_codes", align_bytes=64)
-            scales = keep.tile([P, width], U8, name=f"{tag}_scales", align_bytes=64)
-            nc.vector.quantize_mx(out=codes[:].bitcast(FP8X4), scales=scales[:], in_=grouped[:])
-            return codes, scales
-
-        g1 = [round_slot(raw1, t, t >= 2, "w1") for t in range(4)]
-        q1 = [quantize(g1[t], f"w1_{t}") for t in range(4)]
-
-        raw3 = keep.tile([P, 4, N], F32, name="raw3", tag="raw13", align_bytes=64)
+        w2_rows = w2.rearrange("(p j) c -> p j c", j=4)
+        nc.sync.dma_start(out=raw2_low[:], in_=w2_rows[:, :, 0 : H // 2])
+        nc.sync.dma_start(out=raw2_high[:], in_=w2_rows[:, :, H // 2 : H])
         w3_rows = w3.rearrange("(s j b) c -> b s j c", j=4, b=4)
         for b in range(4):
             nc.sync.dma_start(out=raw3[b:P:4, :, :], in_=w3_rows[b])
 
-        x_code = []
+        x_scale = keep.tile([P, S], U8, name="x_scale", align_bytes=64)
+        nc.vector.tensor_copy(out=x_scale[:], in_=table_scales[:].indirect(offsets[:]))
+        x_code = keep.tile([P, S], U32, name="x_code", align_bytes=64)
         for g in range(S // GATHER):
-            picked = keep.tile([P, GATHER], U32, name=f"x_code{g}", tag=f"w1_slot{g}", align_bytes=64)
-            nc.vector.tensor_copy(out=picked[:], in_=table_words[:].indirect(offsets[:, g * GATHER // 16 : (g + 1) * GATHER // 16]))
-            x_code.append(picked)
+            nc.vector.tensor_copy(out=x_code[:, g * GATHER : (g + 1) * GATHER],
+                                  in_=table_words[:].indirect(offsets[:, g * GATHER // 16 : (g + 1) * GATHER // 16]))
 
-        def project(quantized, u, label):
-            bank = psum.tile([P, 4, P], F32, name=f"{label}{u}", tag=f"bank{u}")
-            words = x_code[u // 2][:, (u % 2) * P : (u % 2 + 1) * P]
+        def round_to_bf16(engine, dst, src):
+            if engine == "scalar":
+                nc.scalar.activation(out=dst, in_=src, func=ACT.Copy)
+            elif engine == "gpsimd":
+                nc.gpsimd.tensor_scalar(out=dst, in0=src, scalar1=1.0, scalar2=0.0, op0=ALU.mult, op1=ALU.add)
+            else:
+                nc.vector.tensor_copy(out=dst, in_=src)
+
+        def round_columns(raw, grouped, slots, engine):
+            src = raw.rearrange("p j (s t b) -> p s t b j", t=4, b=4)[:, :, slots]
+            dst = grouped.rearrange("p t (s b j) -> p s t b j", b=4, j=4)[:, :, slots]
+            round_to_bf16(engine, dst, src)
+
+        def quantize(grouped, label):
+            width = grouped.shape[1] // 4
+            codes = keep.tile([P, width], U32, name=f"{label}_codes", align_bytes=64)
+            scales = keep.tile([P, width], U8, name=f"{label}_scales", align_bytes=64)
+            nc.vector.quantize_mx(out=codes[:].bitcast(FP8X4), scales=scales[:], in_=grouped)
+            return codes, scales
+
+        g1 = keep.tile([P, 4, 512], BF16, name="w1_grouped", align_bytes=64)
+        round_columns(raw1[:], g1[:], slice(2, 4), "scalar")
+        round_columns(raw1[:], g1[:], slice(0, 2), "gpsimd")
+        q1 = [quantize(g1[:, 2 * pair : 2 * pair + 2].rearrange("p t n -> p (t n)"), f"w1_{pair}") for pair in (1, 0)][::-1]
+
+        g2 = keep.tile([P, 4, 512], BF16, name="w2_grouped", align_bytes=64)
+        round_columns(raw2_low[:], g2[:, :, 0:256], slice(0, 4), "scalar")
+        round_columns(raw2_high[:], g2[:, :, 256:512], slice(0, 2), "vector")
+        round_columns(raw2_high[:], g2[:, :, 256:512], slice(2, 4), "scalar")
+        q2 = [quantize(g2[:, 2 * pair : 2 * pair + 2].rearrange("p t n -> p (t n)"), f"w2_{pair}") for pair in range(2)]
+
+        def project(quantized, u, label, bank_number):
+            bank = psum.tile([P, 4, P], F32, name=f"{label}{u}", tag=f"bank{bank_number}")
             cols = slice(u * P, (u + 1) * P)
             for t in range(4):
-                nc.tensor.matmul_mx(out=bank[:, t, :], lhsT=quantized[t][0][:].bitcast(FP8X4), lhsT_scale=quantized[t][1][:],
-                                    rhs=words.bitcast(FP8X4), rhs_scale=x_scale[:, cols], start=True, stop=True)
+                codes, scales = quantized[t // 2]
+                rows = slice((t % 2) * P, (t % 2 + 1) * P)
+                nc.tensor.matmul_mx(out=bank[:, t, :], lhsT=codes[:, rows].bitcast(FP8X4), lhsT_scale=scales[:, rows],
+                                    rhs=x_code[:, cols].bitcast(FP8X4), rhs_scale=x_scale[:, cols], start=True, stop=True)
             return bank
 
-        g3 = keep.tile([P, N * 4], BF16, name="w3_grouped", tag="staged", align_bytes=64)
-        def copy_h(u, h_u):
-            bank = project(q1, u, "h_bank")
-            nc.scalar.copy(out=h_u, in_=bank[:].rearrange("p t (v d) -> p d v t", d=2))
+        def copy_h(u):
+            h_u = reuse.tile([P, 2, 64, 4], F32, name=f"h_sb{u}", offset=2048 * u)
+            bank = project(q1, u, "h_bank", u % 2)
+            nc.scalar.copy(out=h_u[:], in_=bank[:].rearrange("p t (v d) -> p d v t", d=2))
             return h_u
-
-        h_first = keep.tile([P, 2, 64, 4], F32, name="h_first", align_bytes=64)
-        h_sb = [copy_h(0, h_first[:])]
-        g2 = [round_slot(raw2, t, t >= 2, "w2") for t in range(4)]
-        q2 = [quantize(g2[t], f"w2_{t}") for t in range(4)]
-        h_mid = keep.tile([P, 4, 2, 64, 4], F32, name="h_mid", tag="raw2", align_bytes=64)
-        h_sb.extend(copy_h(u, h_mid[:, u - 1]) for u in range(1, 5))
-        nc.scalar.copy(out=g3[:].rearrange("p (t m j) -> p m t j", t=4, j=4), in_=raw3[:].rearrange("p j (m t) -> p m t j", t=4))
-        h_last = keep.tile([P, 3, 2, 64, 4], F32, name="h_last", tag="raw13", align_bytes=64)
-        h_sb.extend(copy_h(u, h_last[:, u - 5]) for u in range(5, UNITS))
 
         y_words = keep.tile([P, V], U32, name="y_words", align_bytes=64)
         y_scales = keep.tile([P, V], U8, name="y_scales", align_bytes=64)
         out_rows = out_0.rearrange("(p t) v -> p t v", t=4)
         out_words = out_1[0].rearrange("p c r -> p (c r)").bitcast(I32)
 
-        zq = []
-        for q in range(QUARTERS):
-            if q == 1:
-                w3_codes, w3_scales = quantize(g3, "w3")
-            z = keep.tile([P, 512], BF16, name=f"z{q}", tag="staged" if q == 2 else f"z{q}", align_bytes=64)
+        def pair_sums(q):
+            z = keep.tile([P, 512], BF16, name=f"z{q}", tag="staged1" if q == 2 else f"z{q}", align_bytes=64)
             for a in range(2):
                 u = 2 * q + a
+                e_bank = project(q2, u, "e_bank", 2 + u % 2)
                 prod = ring.tile([P, 2, 256], F32, name="prod", align_bytes=64)
-                bank = project(q2, u, "e_bank")
                 nc.vector.tensor_tensor(out=prod[:].rearrange("p d (v t) -> p d v t", t=4),
-                                        in0=bank[:].rearrange("p t (v d) -> p d v t", d=2),
+                                        in0=e_bank[:].rearrange("p t (v d) -> p d v t", d=2),
                                         in1=h_sb[u][:, ::-1], op=ALU.mult)
-                nc.vector.tensor_tensor(out=z[:, a * 256 : (a + 1) * 256], in0=prod[:, 0, :], in1=prod[:, 1, :], op=ALU.add)
-            zq.append(quantize(z, f"z{q}"))
+                adder = nc.gpsimd if u < 4 else nc.vector
+                adder.tensor_tensor(out=z[:, a * 256 : (a + 1) * 256], in0=prod[:, 0, :], in1=prod[:, 1, :], op=ALU.add)
+            return quantize(z[:], f"z{q}")
+
+        h_sb = [copy_h(u) for u in range(4)]
+        zq = [pair_sums(0)]
+        w3_src = raw3[:].rearrange("p j (m t) -> p m t j", t=4)
+        q3 = []
+        for pair, engine in enumerate(("gpsimd", "scalar")):
+            g3 = keep.tile([P, 1024], BF16, name=f"w3_grouped{pair}", tag=f"staged{pair}", align_bytes=64)
+            round_to_bf16(engine, g3[:].rearrange("p (t m j) -> p m t j", t=2, j=4), w3_src[:, :, 2 * pair : 2 * pair + 2])
+            q3.append(quantize(g3[:], f"w3_{pair}"))
+        h_sb.extend(copy_h(u) for u in range(4, UNITS))
+        zq.extend(pair_sums(q) for q in range(1, QUARTERS))
 
         for q in range(QUARTERS):
             cols = slice(q * P, (q + 1) * P)
-            bank = psum.tile([P, 4, P], F32, name=f"y_bank{q}", tag=f"bank{q}")
+            bank = psum.tile([P, 4, P], F32, name=f"y_bank{q}", tag=f"bank{4 + q}")
             for t in range(4):
-                nc.tensor.matmul_mx(out=bank[:, t, :], lhsT=w3_codes[:, t * P : (t + 1) * P].bitcast(FP8X4), lhsT_scale=w3_scales[:, t * P : (t + 1) * P],
+                codes, scales = q3[t // 2]
+                rows = slice((t % 2) * P, (t % 2 + 1) * P)
+                nc.tensor.matmul_mx(out=bank[:, t, :], lhsT=codes[:, rows].bitcast(FP8X4), lhsT_scale=scales[:, rows],
                                     rhs=zq[q][0][:].bitcast(FP8X4), rhs_scale=zq[q][1][:], start=True, stop=True)
             y16 = keep.tile([P, 512], BF16, name=f"y16_{q}", align_bytes=64)
             y32 = keep.tile([P, 4, P], F32, name=f"y32_{q}", align_bytes=64)

@@ -17,6 +17,10 @@ K, T, S, V, H, N = 512, 2048, 1024, 512, 512, 512
 FLOPS = 2 * K * H * S * 2 + 2 * H * N * V
 UNITS = 8
 QUARTERS = 4
+H_OFFSET = (4096, 6144, 0, 2048, 16384, 18432, 8192, 10240)
+H_BANK = (0, 1, 2, 3)
+E_BANK = (4, 5, 6, 7)
+Y_BANK = (2, 3, 0, 1)
 GATHER = 512
 
 
@@ -24,7 +28,6 @@ def tile_picked_zfm_relu_po_kernel(tc, x_words, x_scales, w1, w2, w3, offs, out_
     nc = tc.nc
     with ExitStack() as ctx:
         keep = ctx.enter_context(tc.tile_pool(name="keep", bufs=1))
-        ring = ctx.enter_context(tc.tile_pool(name="ring", bufs=6))
         reuse = ctx.enter_context(tc.tile_pool(name="reuse", bufs=1))
         psum = ctx.enter_context(tc.psum_pool(name="psum", bufs=1))
 
@@ -85,8 +88,7 @@ def tile_picked_zfm_relu_po_kernel(tc, x_words, x_scales, w1, w2, w3, offs, out_
 
         g2 = keep.tile([P, 4, 512], BF16, name="w2_grouped", align_bytes=64)
         round_columns(raw2_low[:], g2[:, :, 0:256], slice(0, 4), "scalar")
-        round_columns(raw2_high[:], g2[:, :, 256:512], slice(0, 2), "vector")
-        round_columns(raw2_high[:], g2[:, :, 256:512], slice(2, 4), "scalar")
+        round_columns(raw2_high[:], g2[:, :, 256:512], slice(0, 4), "vector")
         q2 = [quantize(g2[:, 2 * pair : 2 * pair + 2].rearrange("p t n -> p (t n)"), f"w2_{pair}") for pair in range(2)]
 
         def project(quantized, u, label, bank_number):
@@ -99,9 +101,12 @@ def tile_picked_zfm_relu_po_kernel(tc, x_words, x_scales, w1, w2, w3, offs, out_
                                     rhs=x_code[:, cols].bitcast(FP8X4), rhs_scale=x_scale[:, cols], start=True, stop=True)
             return bank
 
+        def project_e(u):
+            return project(q2, u, "e_bank", E_BANK[u % 4])
+
         def copy_h(u):
-            h_u = reuse.tile([P, 2, 64, 4], F32, name=f"h_sb{u}", offset=2048 * u)
-            bank = project(q1, u, "h_bank", u % 2)
+            h_u = reuse.tile([P, 2, 64, 4], F32, name=f"h_sb{u}", offset=H_OFFSET[u])
+            bank = project(q1, u, "h_bank", H_BANK[u % 4])
             nc.scalar.copy(out=h_u[:], in_=bank[:].rearrange("p t (v d) -> p d v t", d=2))
             return h_u
 
@@ -111,32 +116,44 @@ def tile_picked_zfm_relu_po_kernel(tc, x_words, x_scales, w1, w2, w3, offs, out_
         out_words = out_1[0].rearrange("p c r -> p (c r)").bitcast(I32)
 
         def pair_sums(q):
-            z = keep.tile([P, 512], BF16, name=f"z{q}", tag="staged1" if q == 2 else f"z{q}", align_bytes=64)
+            if q == 0:
+                z = reuse.tile([P, 2, 256], BF16, name="z0", offset=20480, align_bytes=64)
+            else:
+                z = keep.tile([P, 2, 256], BF16, name=f"z{q}", align_bytes=64)
+            if q == 2:
+                prod = reuse.tile([P, 2, 2, 256], F32, name="prod_tied", offset=21504, align_bytes=64)
+            else:
+                prod = keep.tile([P, 2, 2, 256], F32, name=f"prod{q}", align_bytes=64)
             for a in range(2):
                 u = 2 * q + a
-                e_bank = project(q2, u, "e_bank", 2 + u % 2)
-                prod = ring.tile([P, 2, 256], F32, name="prod", align_bytes=64)
-                nc.vector.tensor_tensor(out=prod[:].rearrange("p d (v t) -> p d v t", t=4),
+                e_bank = e_early[u] if u < 4 else project_e(u)
+                nc.vector.tensor_tensor(out=prod[:, a].rearrange("p d (v t) -> p d v t", t=4),
                                         in0=e_bank[:].rearrange("p t (v d) -> p d v t", d=2),
                                         in1=h_sb[u][:, ::-1], op=ALU.mult)
-                adder = nc.gpsimd if u < 4 else nc.vector
-                adder.tensor_tensor(out=z[:, a * 256 : (a + 1) * 256], in0=prod[:, 0, :], in1=prod[:, 1, :], op=ALU.add)
-            return quantize(z[:], f"z{q}")
+                if q == QUARTERS - 1:
+                    nc.vector.tensor_tensor(out=z[:, a, :], in0=prod[:, a, 0, :], in1=prod[:, a, 1, :], op=ALU.add)
+            if q < QUARTERS - 1:
+                adder = nc.gpsimd if q < 2 else nc.vector
+                adder.tensor_tensor(out=z[:], in0=prod[:, :, 0, :], in1=prod[:, :, 1, :], op=ALU.add)
+            return quantize(z[:].rearrange("p a n -> p (a n)"), f"z{q}")
 
         h_sb = [copy_h(u) for u in range(4)]
-        zq = [pair_sums(0)]
+        e_early = [project_e(0), project_e(1)]
+        for u in (4, 5):
+            h_sb.append(copy_h(u))
+            e_early.append(project_e(u - 2))
         w3_src = raw3[:].rearrange("p j (m t) -> p m t j", t=4)
         q3 = []
         for pair, engine in enumerate(("gpsimd", "scalar")):
-            g3 = keep.tile([P, 1024], BF16, name=f"w3_grouped{pair}", tag=f"staged{pair}", align_bytes=64)
+            g3 = reuse.tile([P, 1024], BF16, name=f"w3_grouped{pair}", offset=(20480, 25600)[pair], align_bytes=64)
             round_to_bf16(engine, g3[:].rearrange("p (t m j) -> p m t j", t=2, j=4), w3_src[:, :, 2 * pair : 2 * pair + 2])
             q3.append(quantize(g3[:], f"w3_{pair}"))
-        h_sb.extend(copy_h(u) for u in range(4, UNITS))
-        zq.extend(pair_sums(q) for q in range(1, QUARTERS))
+        h_sb.extend(copy_h(u) for u in range(6, UNITS))
+        zq = [pair_sums(q) for q in range(QUARTERS)]
 
         for q in range(QUARTERS):
             cols = slice(q * P, (q + 1) * P)
-            bank = psum.tile([P, 4, P], F32, name=f"y_bank{q}", tag=f"bank{4 + q}")
+            bank = psum.tile([P, 4, P], F32, name=f"y_bank{q}", tag=f"bank{Y_BANK[q]}")
             for t in range(4):
                 codes, scales = q3[t // 2]
                 rows = slice((t % 2) * P, (t % 2 + 1) * P)
@@ -144,10 +161,10 @@ def tile_picked_zfm_relu_po_kernel(tc, x_words, x_scales, w1, w2, w3, offs, out_
                                     rhs=zq[q][0][:].bitcast(FP8X4), rhs_scale=zq[q][1][:], start=True, stop=True)
             y16 = keep.tile([P, 512], BF16, name=f"y16_{q}", align_bytes=64)
             y32 = keep.tile([P, 4, P], F32, name=f"y32_{q}", align_bytes=64)
-            if q >= 2:
-                nc.scalar.activation(out=y16[:].rearrange("p (v t) -> p v t", t=4), in_=bank[:].rearrange("p t v -> p v t"), func=ACT.Relu)
             nc.scalar.activation(out=y32[:], in_=bank[:], func=ACT.Relu)
-            if q < 2:
+            if q < 1:
+                nc.scalar.activation(out=y16[:].rearrange("p (v t) -> p v t", t=4), in_=bank[:].rearrange("p t v -> p v t"), func=ACT.Relu)
+            else:
                 nc.vector.tensor_copy(out=y16[:].rearrange("p (v t) -> p v t", t=4), in_=y32[:].rearrange("p t v -> p v t"))
             nc.vector.quantize_mx(out=y_words[:, cols].bitcast(FP8X4), scales=y_scales[:, cols], in_=y16[:])
             nc.sync.dma_start(out=out_rows[:, :, cols], in_=y32[:])

@@ -15,64 +15,72 @@ ALU = mybir.AluOpType
 P = 128
 K, T, S, V, H, N = 512, 2048, 1024, 512, 512, 512
 FLOPS = 2 * K * H * S * 2 + 2 * H * N * V
-UNITS = 8
-QUARTERS = 4
-H_OFFSET = (4096, 6144, 0, 2048, 16384, 18432, 8192, 10240)
-H_BANK = (0, 1, 2, 3)
-E_BANK = (4, 5, 6, 7)
+UNITS = S // P
+QUARTERS = V // P
+SLOT_PAIRS = (slice(0, 2), slice(2, 4))
+
+RING = 4
 Y_BANK = (2, 3, 0, 1)
-GATHER = 512
+
+GPSIMD_ADD_QUARTERS = 1
+SCALAR_ROUND_QUARTERS = 2
+
+H_BYTES = 2048
+RAW2_HIGH_AT = 0
+RAW2_LOW_AT = 2 * H_BYTES
+RAW3_AT = 4 * H_BYTES
+H_MIDDLE_AT = 8 * H_BYTES
+W3_FIRST_AT = 10 * H_BYTES
+PRODUCTS_1_AT = W3_FIRST_AT + H_BYTES // 2
+W3_SECOND_AT = PRODUCTS_1_AT + 2 * H_BYTES
+H_PAIR_AT = (RAW2_LOW_AT, RAW2_HIGH_AT, H_MIDDLE_AT, RAW3_AT)
 
 
 def tile_picked_zfm_relu_po_kernel(tc, x_words, x_scales, w1, w2, w3, offs, out_0, out_1, out_2):
     nc = tc.nc
     with ExitStack() as ctx:
         keep = ctx.enter_context(tc.tile_pool(name="keep", bufs=1))
-        reuse = ctx.enter_context(tc.tile_pool(name="reuse", bufs=1))
+        shared = ctx.enter_context(tc.tile_pool(name="shared", bufs=1))
         psum = ctx.enter_context(tc.psum_pool(name="psum", bufs=1))
 
         offsets = keep.tile([P, S // 16], U16, name="offsets")
         table_words = keep.tile([P, T], U32, name="table_words", align_bytes=64)
         table_scales = keep.tile([P, T], U8, name="table_scales", align_bytes=64)
         raw1 = keep.tile([P, 4, H], F32, name="raw1", align_bytes=64)
-        raw2_low = reuse.tile([P, 4, H // 2], F32, name="raw2_low", offset=4096)
-        raw2_high = reuse.tile([P, 4, H // 2], F32, name="raw2_high", offset=0)
-        raw3 = reuse.tile([P, 4, N], F32, name="raw3", offset=8192)
+        raw2_low = shared.tile([P, 4, H // 2], F32, name="raw2_low", offset=RAW2_LOW_AT)
+        raw2_high = shared.tile([P, 4, H // 2], F32, name="raw2_high", offset=RAW2_HIGH_AT)
+        raw3 = shared.tile([P, 4, N], F32, name="raw3", offset=RAW3_AT)
 
         nc.vector.memset(table_scales[:].bitcast(I32), 0)
         nc.sync.dma_start(out=offsets[:], in_=offs)
         words_in = x_words[0].rearrange("p c r -> p (c r)").bitcast(I32)
-        nc.sync.dma_start(out=table_words[:, 0:1024].bitcast(I32), in_=words_in[:, 0:1024])
-        for q in range(4):
-            nc.sync.dma_start(out=table_scales[32 * q : 32 * q + 4, :].bitcast(I32), in_=x_scales[0, 4 * q : 4 * q + 4, :].bitcast(I32))
-        nc.sync.dma_start(out=table_words[:, 1024:T].bitcast(I32), in_=words_in[:, 1024:T])
+        nc.sync.dma_start(out=table_words[:, 0 : T // 2].bitcast(I32), in_=words_in[:, 0 : T // 2])
+        for quadrant in range(4):
+            nc.sync.dma_start(out=table_scales[32 * quadrant : 32 * quadrant + 4, :].bitcast(I32),
+                              in_=x_scales[0, 4 * quadrant : 4 * quadrant + 4, :].bitcast(I32))
+        nc.sync.dma_start(out=table_words[:, T // 2 : T].bitcast(I32), in_=words_in[:, T // 2 : T])
         nc.sync.dma_start(out=raw1[:], in_=w1.rearrange("(p j) c -> p j c", j=4))
         w2_rows = w2.rearrange("(p j) c -> p j c", j=4)
         nc.sync.dma_start(out=raw2_low[:], in_=w2_rows[:, :, 0 : H // 2])
         nc.sync.dma_start(out=raw2_high[:], in_=w2_rows[:, :, H // 2 : H])
-        w3_rows = w3.rearrange("(s j b) c -> b s j c", j=4, b=4)
-        for b in range(4):
-            nc.sync.dma_start(out=raw3[b:P:4, :, :], in_=w3_rows[b])
+        nc.sync.dma_start(out=raw3[:], in_=w3.rearrange("(p j) c -> p j c", j=4))
 
         x_scale = keep.tile([P, S], U8, name="x_scale", align_bytes=64)
         nc.vector.tensor_copy(out=x_scale[:], in_=table_scales[:].indirect(offsets[:]))
         x_code = keep.tile([P, S], U32, name="x_code", align_bytes=64)
-        for g in range(S // GATHER):
-            nc.vector.tensor_copy(out=x_code[:, g * GATHER : (g + 1) * GATHER],
-                                  in_=table_words[:].indirect(offsets[:, g * GATHER // 16 : (g + 1) * GATHER // 16]))
+        for first in range(0, S, S // 2):
+            nc.vector.tensor_copy(out=x_code[:, first : first + S // 2],
+                                  in_=table_words[:].indirect(offsets[:, first // 16 : (first + S // 2) // 16]))
 
-        def round_to_bf16(engine, dst, src):
+        def round_slots(engine, raw, grouped, slots):
+            src = raw.rearrange("p j (m t) -> p m t j", t=4)[:, :, slots]
+            dst = grouped.rearrange("p t (m j) -> p m t j", j=4)
             if engine == "scalar":
                 nc.scalar.activation(out=dst, in_=src, func=ACT.Copy)
             elif engine == "gpsimd":
                 nc.gpsimd.tensor_scalar(out=dst, in0=src, scalar1=1.0, scalar2=0.0, op0=ALU.mult, op1=ALU.add)
             else:
                 nc.vector.tensor_copy(out=dst, in_=src)
-
-        def round_columns(raw, grouped, slots, engine):
-            src = raw.rearrange("p j (s t b) -> p s t b j", t=4, b=4)[:, :, slots]
-            dst = grouped.rearrange("p t (s b j) -> p s t b j", b=4, j=4)[:, :, slots]
-            round_to_bf16(engine, dst, src)
 
         def quantize(grouped, label):
             width = grouped.shape[1] // 4
@@ -81,34 +89,39 @@ def tile_picked_zfm_relu_po_kernel(tc, x_words, x_scales, w1, w2, w3, offs, out_
             nc.vector.quantize_mx(out=codes[:].bitcast(FP8X4), scales=scales[:], in_=grouped)
             return codes, scales
 
-        g1 = keep.tile([P, 4, 512], BF16, name="w1_grouped", align_bytes=64)
-        round_columns(raw1[:], g1[:], slice(2, 4), "scalar")
-        round_columns(raw1[:], g1[:], slice(0, 2), "gpsimd")
-        q1 = [quantize(g1[:, 2 * pair : 2 * pair + 2].rearrange("p t n -> p (t n)"), f"w1_{pair}") for pair in (1, 0)][::-1]
-
-        g2 = keep.tile([P, 4, 512], BF16, name="w2_grouped", align_bytes=64)
-        round_columns(raw2_low[:], g2[:, :, 0:256], slice(0, 4), "scalar")
-        round_columns(raw2_high[:], g2[:, :, 256:512], slice(0, 4), "vector")
-        q2 = [quantize(g2[:, 2 * pair : 2 * pair + 2].rearrange("p t n -> p (t n)"), f"w2_{pair}") for pair in range(2)]
-
-        def project(quantized, u, label, bank_number):
-            bank = psum.tile([P, 4, P], F32, name=f"{label}{u}", tag=f"bank{bank_number}")
-            cols = slice(u * P, (u + 1) * P)
+        def multiply(weight, codes, scales, label, bank_number):
+            bank = psum.tile([P, 4, P], F32, name=label, tag=f"bank{bank_number}")
             for t in range(4):
-                codes, scales = quantized[t // 2]
-                rows = slice((t % 2) * P, (t % 2 + 1) * P)
-                nc.tensor.matmul_mx(out=bank[:, t, :], lhsT=codes[:, rows].bitcast(FP8X4), lhsT_scale=scales[:, rows],
-                                    rhs=x_code[:, cols].bitcast(FP8X4), rhs_scale=x_scale[:, cols], start=True, stop=True)
+                pair_codes, pair_scales = weight[t // 2]
+                places = slice((t % 2) * P, (t % 2 + 1) * P)
+                nc.tensor.matmul_mx(out=bank[:, t, :], lhsT=pair_codes[:, places].bitcast(FP8X4), lhsT_scale=pair_scales[:, places],
+                                    rhs=codes.bitcast(FP8X4), rhs_scale=scales, start=True, stop=True)
             return bank
 
-        def project_e(u):
-            return project(q2, u, "e_bank", E_BANK[u % 4])
+        w1_grouped = keep.tile([P, 4, 4 * P], BF16, name="w1_grouped", align_bytes=64)
+        round_slots("scalar", raw1[:], w1_grouped[:, SLOT_PAIRS[1]], SLOT_PAIRS[1])
+        round_slots("gpsimd", raw1[:], w1_grouped[:, SLOT_PAIRS[0]], SLOT_PAIRS[0])
+        w1_second = quantize(w1_grouped[:, SLOT_PAIRS[1]].rearrange("p t n -> p (t n)"), "w1_1")
+        w1_first = quantize(w1_grouped[:, SLOT_PAIRS[0]].rearrange("p t n -> p (t n)"), "w1_0")
+        w1_mx = (w1_first, w1_second)
+
+        w2_grouped = keep.tile([P, 4, 4 * P], BF16, name="w2_grouped", align_bytes=64)
+        for slots in SLOT_PAIRS:
+            round_slots("scalar", raw2_low[:], w2_grouped[:, slots, 0 : 2 * P], slots)
+        for slots in SLOT_PAIRS:
+            round_slots("vector", raw2_high[:], w2_grouped[:, slots, 2 * P : 4 * P], slots)
+        w2_mx = [quantize(w2_grouped[:, slots].rearrange("p t n -> p (t n)"), f"w2_{pair}") for pair, slots in enumerate(SLOT_PAIRS)]
 
         def copy_h(u):
-            h_u = reuse.tile([P, 2, 64, 4], F32, name=f"h_sb{u}", offset=H_OFFSET[u])
-            bank = project(q1, u, "h_bank", H_BANK[u % 4])
+            h_u = shared.tile([P, 2, P // 2, 4], F32, name=f"h_sb{u}", offset=H_PAIR_AT[u // 2] + (u % 2) * H_BYTES)
+            entries = slice(u * P, (u + 1) * P)
+            bank = multiply(w1_mx, x_code[:, entries], x_scale[:, entries], f"h_bank{u}", u % RING)
             nc.scalar.copy(out=h_u[:], in_=bank[:].rearrange("p t (v d) -> p d v t", d=2))
             return h_u
+
+        def project_e(u):
+            entries = slice(u * P, (u + 1) * P)
+            return multiply(w2_mx, x_code[:, entries], x_scale[:, entries], f"e_bank{u}", RING + u % RING)
 
         y_words = keep.tile([P, V], U32, name="y_words", align_bytes=64)
         y_scales = keep.tile([P, V], U8, name="y_scales", align_bytes=64)
@@ -117,60 +130,57 @@ def tile_picked_zfm_relu_po_kernel(tc, x_words, x_scales, w1, w2, w3, offs, out_
 
         def pair_sums(q):
             if q == 0:
-                z = reuse.tile([P, 2, 256], BF16, name="z0", offset=20480, align_bytes=64)
+                z = shared.tile([P, 2, 2 * P], BF16, name="z0", offset=W3_FIRST_AT, align_bytes=64)
             else:
-                z = keep.tile([P, 2, 256], BF16, name=f"z{q}", align_bytes=64)
-            if q == 2:
-                prod = reuse.tile([P, 2, 2, 256], F32, name="prod_tied", offset=21504, align_bytes=64)
+                z = keep.tile([P, 2, 2 * P], BF16, name=f"z{q}", align_bytes=64)
+            if q == 1:
+                products = shared.tile([P, 2, 2, 2 * P], F32, name="products1", offset=PRODUCTS_1_AT, align_bytes=64)
             else:
-                prod = keep.tile([P, 2, 2, 256], F32, name=f"prod{q}", align_bytes=64)
+                products = keep.tile([P, 2, 2, 2 * P], F32, name=f"products{q}", align_bytes=64)
             for a in range(2):
                 u = 2 * q + a
-                e_bank = e_early[u] if u < 4 else project_e(u)
-                nc.vector.tensor_tensor(out=prod[:, a].rearrange("p d (v t) -> p d v t", t=4),
+                e_bank = e_first_round[u] if u < RING else project_e(u)
+                nc.vector.tensor_tensor(out=products[:, a].rearrange("p d (v t) -> p d v t", t=4),
                                         in0=e_bank[:].rearrange("p t (v d) -> p d v t", d=2),
                                         in1=h_sb[u][:, ::-1], op=ALU.mult)
                 if q == QUARTERS - 1:
-                    nc.vector.tensor_tensor(out=z[:, a, :], in0=prod[:, a, 0, :], in1=prod[:, a, 1, :], op=ALU.add)
+                    nc.vector.tensor_tensor(out=z[:, a, :], in0=products[:, a, 0, :], in1=products[:, a, 1, :], op=ALU.add)
             if q < QUARTERS - 1:
-                adder = nc.gpsimd if q < 2 else nc.vector
-                adder.tensor_tensor(out=z[:], in0=prod[:, :, 0, :], in1=prod[:, :, 1, :], op=ALU.add)
+                adder = nc.gpsimd if q < GPSIMD_ADD_QUARTERS else nc.vector
+                adder.tensor_tensor(out=z[:], in0=products[:, :, 0, :], in1=products[:, :, 1, :], op=ALU.add)
             return quantize(z[:].rearrange("p a n -> p (a n)"), f"z{q}")
 
-        h_sb = [copy_h(u) for u in range(4)]
-        e_early = [project_e(0), project_e(1)]
-        for u in (4, 5):
+        h_sb = [copy_h(u) for u in range(RING)]
+        e_first_round = [project_e(0), project_e(1)]
+        for u in range(RING, RING + 2):
             h_sb.append(copy_h(u))
-            e_early.append(project_e(u - 2))
-        w3_src = raw3[:].rearrange("p j (m t) -> p m t j", t=4)
-        q3 = []
-        for pair, engine in enumerate(("gpsimd", "scalar")):
-            g3 = reuse.tile([P, 1024], BF16, name=f"w3_grouped{pair}", offset=(20480, 25600)[pair], align_bytes=64)
-            round_to_bf16(engine, g3[:].rearrange("p (t m j) -> p m t j", t=2, j=4), w3_src[:, :, 2 * pair : 2 * pair + 2])
-            q3.append(quantize(g3[:], f"w3_{pair}"))
-        h_sb.extend(copy_h(u) for u in range(6, UNITS))
-        zq = [pair_sums(q) for q in range(QUARTERS)]
+            e_first_round.append(project_e(u - 2))
+
+        w3_mx = []
+        for pair, (engine, at) in enumerate((("gpsimd", W3_FIRST_AT), ("scalar", W3_SECOND_AT))):
+            w3_grouped = shared.tile([P, 2, 4 * P], BF16, name=f"w3_grouped{pair}", offset=at, align_bytes=64)
+            round_slots(engine, raw3[:], w3_grouped[:], SLOT_PAIRS[pair])
+            w3_mx.append(quantize(w3_grouped[:].rearrange("p t n -> p (t n)"), f"w3_{pair}"))
+        h_sb.extend(copy_h(u) for u in range(RING + 2, UNITS))
+        z_mx = [pair_sums(q) for q in range(QUARTERS)]
 
         for q in range(QUARTERS):
-            cols = slice(q * P, (q + 1) * P)
-            bank = psum.tile([P, 4, P], F32, name=f"y_bank{q}", tag=f"bank{Y_BANK[q]}")
-            for t in range(4):
-                codes, scales = q3[t // 2]
-                rows = slice((t % 2) * P, (t % 2 + 1) * P)
-                nc.tensor.matmul_mx(out=bank[:, t, :], lhsT=codes[:, rows].bitcast(FP8X4), lhsT_scale=scales[:, rows],
-                                    rhs=zq[q][0][:].bitcast(FP8X4), rhs_scale=zq[q][1][:], start=True, stop=True)
-            y16 = keep.tile([P, 512], BF16, name=f"y16_{q}", align_bytes=64)
+            records = slice(q * P, (q + 1) * P)
+            z_codes, z_scales = z_mx[q]
+            bank = multiply(w3_mx, z_codes[:], z_scales[:], f"y_bank{q}", Y_BANK[q])
+            y16 = keep.tile([P, 4 * P], BF16, name=f"y16_{q}", align_bytes=64)
             y32 = keep.tile([P, 4, P], F32, name=f"y32_{q}", align_bytes=64)
             nc.scalar.activation(out=y32[:], in_=bank[:], func=ACT.Relu)
-            if q < 1:
+            if q < SCALAR_ROUND_QUARTERS:
                 nc.scalar.activation(out=y16[:].rearrange("p (v t) -> p v t", t=4), in_=bank[:].rearrange("p t v -> p v t"), func=ACT.Relu)
             else:
                 nc.vector.tensor_copy(out=y16[:].rearrange("p (v t) -> p v t", t=4), in_=y32[:].rearrange("p t v -> p v t"))
-            nc.vector.quantize_mx(out=y_words[:, cols].bitcast(FP8X4), scales=y_scales[:, cols], in_=y16[:])
-            nc.sync.dma_start(out=out_rows[:, :, cols], in_=y32[:])
-            if q == 2:
-                nc.sync.dma_start(out=out_words[:, 0 : 3 * P], in_=y_words[:, 0 : 3 * P].bitcast(I32))
-        nc.sync.dma_start(out=out_words[:, 3 * P : V], in_=y_words[:, 3 * P : V].bitcast(I32))
-        for q in range(4):
-            queue = nc.sync if q % 2 == 0 else nc.scalar
-            queue.dma_start(out=out_2[0, 4 * q : 4 * q + 4, :].bitcast(I32), in_=y_scales[32 * q : 32 * q + 4, :].bitcast(I32))
+            nc.vector.quantize_mx(out=y_words[:, records].bitcast(FP8X4), scales=y_scales[:, records], in_=y16[:])
+            nc.sync.dma_start(out=out_rows[:, :, records], in_=y32[:])
+            if q == QUARTERS - 2:
+                nc.sync.dma_start(out=out_words[:, 0 : V - P], in_=y_words[:, 0 : V - P].bitcast(I32))
+        nc.sync.dma_start(out=out_words[:, V - P : V], in_=y_words[:, V - P : V].bitcast(I32))
+        for quadrant in range(4):
+            queue = nc.sync if quadrant % 2 == 0 else nc.scalar
+            queue.dma_start(out=out_2[0, 4 * quadrant : 4 * quadrant + 4, :].bitcast(I32),
+                            in_=y_scales[32 * quadrant : 32 * quadrant + 4, :].bitcast(I32))

from contextlib import ExitStack

import concourse.mybir as mybir

F32 = mybir.dt.float32
BF16 = mybir.dt.bfloat16
I32 = mybir.dt.int32
U32 = mybir.dt.uint32
U16 = mybir.dt.uint16
U8 = mybir.dt.uint8
FP8X4 = mybir.dt.float8_e4m3fn_x4
ACT = mybir.ActivationFunctionType
ALU = mybir.AluOpType

P = 128
K, T, S, V, H, N = 512, 2048, 1024, 512, 512, 512
FLOPS = 2 * K * H * S * 2 + 2 * H * N * V
UNITS = S // P
QUARTERS = V // P
SLOT_PAIRS = (slice(0, 2), slice(2, 4))

RING = 4
Y_BANK = (2, 3, 0, 1)

GPSIMD_ADD_QUARTERS = 1
SCALAR_ROUND_QUARTERS = 2

H_BYTES = 2048
RAW2_HIGH_AT = 0
RAW2_LOW_AT = 2 * H_BYTES
RAW3_AT = 4 * H_BYTES
H_MIDDLE_AT = 8 * H_BYTES
W3_FIRST_AT = 10 * H_BYTES
PRODUCTS_1_AT = W3_FIRST_AT + H_BYTES // 2
W3_SECOND_AT = PRODUCTS_1_AT + 2 * H_BYTES
H_PAIR_AT = (RAW2_LOW_AT, RAW2_HIGH_AT, H_MIDDLE_AT, RAW3_AT)


def tile_picked_zfm_relu_po_kernel(tc, x_words, x_scales, w1, w2, w3, offs, out_0, out_1, out_2):
    nc = tc.nc
    with ExitStack() as ctx:
        keep = ctx.enter_context(tc.tile_pool(name="keep", bufs=1))
        shared = ctx.enter_context(tc.tile_pool(name="shared", bufs=1))
        psum = ctx.enter_context(tc.psum_pool(name="psum", bufs=1))

        offsets = keep.tile([P, S // 16], U16, name="offsets")
        table_words = keep.tile([P, T], U32, name="table_words", align_bytes=64)
        table_scales = keep.tile([P, T], U8, name="table_scales", align_bytes=64)
        raw1 = keep.tile([P, 4, H], F32, name="raw1", align_bytes=64)
        raw2_low = shared.tile([P, 4, H // 2], F32, name="raw2_low", offset=RAW2_LOW_AT)
        raw2_high = shared.tile([P, 4, H // 2], F32, name="raw2_high", offset=RAW2_HIGH_AT)
        raw3 = shared.tile([P, 4, N], F32, name="raw3", offset=RAW3_AT)

        nc.vector.memset(table_scales[:].bitcast(I32), 0)
        nc.sync.dma_start(out=offsets[:], in_=offs)
        words_in = x_words[0].rearrange("p c r -> p (c r)").bitcast(I32)
        nc.sync.dma_start(out=table_words[:, 0 : T // 2].bitcast(I32), in_=words_in[:, 0 : T // 2])
        for quadrant in range(4):
            nc.sync.dma_start(out=table_scales[32 * quadrant : 32 * quadrant + 4, :].bitcast(I32),
                              in_=x_scales[0, 4 * quadrant : 4 * quadrant + 4, :].bitcast(I32))
        nc.sync.dma_start(out=table_words[:, T // 2 : T].bitcast(I32), in_=words_in[:, T // 2 : T])
        nc.sync.dma_start(out=raw1[:], in_=w1.rearrange("(p j) c -> p j c", j=4))
        w2_rows = w2.rearrange("(p j) c -> p j c", j=4)
        nc.sync.dma_start(out=raw2_low[:], in_=w2_rows[:, :, 0 : H // 2])
        nc.sync.dma_start(out=raw2_high[:], in_=w2_rows[:, :, H // 2 : H])
        nc.sync.dma_start(out=raw3[:], in_=w3.rearrange("(p j) c -> p j c", j=4))

        x_scale = keep.tile([P, S], U8, name="x_scale", align_bytes=64)
        nc.vector.tensor_copy(out=x_scale[:], in_=table_scales[:].indirect(offsets[:]))
        x_code = keep.tile([P, S], U32, name="x_code", align_bytes=64)
        for first in range(0, S, S // 2):
            nc.vector.tensor_copy(out=x_code[:, first : first + S // 2],
                                  in_=table_words[:].indirect(offsets[:, first // 16 : (first + S // 2) // 16]))

        def round_slots(engine, raw, grouped, slots):
            src = raw.rearrange("p j (m t) -> p m t j", t=4)[:, :, slots]
            dst = grouped.rearrange("p t (m j) -> p m t j", j=4)
            if engine == "scalar":
                nc.scalar.activation(out=dst, in_=src, func=ACT.Copy)
            elif engine == "gpsimd":
                nc.gpsimd.tensor_scalar(out=dst, in0=src, scalar1=1.0, scalar2=0.0, op0=ALU.mult, op1=ALU.add)
            else:
                nc.vector.tensor_copy(out=dst, in_=src)

        def quantize(grouped, label):
            width = grouped.shape[1] // 4
            codes = keep.tile([P, width], U32, name=f"{label}_codes", align_bytes=64)
            scales = keep.tile([P, width], U8, name=f"{label}_scales", align_bytes=64)
            nc.vector.quantize_mx(out=codes[:].bitcast(FP8X4), scales=scales[:], in_=grouped)
            return codes, scales

        def multiply(weight, codes, scales, label, bank_number):
            bank = psum.tile([P, 4, P], F32, name=label, tag=f"bank{bank_number}")
            for t in range(4):
                pair_codes, pair_scales = weight[t // 2]
                places = slice((t % 2) * P, (t % 2 + 1) * P)
                nc.tensor.matmul_mx(out=bank[:, t, :], lhsT=pair_codes[:, places].bitcast(FP8X4), lhsT_scale=pair_scales[:, places],
                                    rhs=codes.bitcast(FP8X4), rhs_scale=scales, start=True, stop=True)
            return bank

        w1_grouped = keep.tile([P, 4, 4 * P], BF16, name="w1_grouped", align_bytes=64)
        round_slots("scalar", raw1[:], w1_grouped[:, SLOT_PAIRS[1]], SLOT_PAIRS[1])
        round_slots("gpsimd", raw1[:], w1_grouped[:, SLOT_PAIRS[0]], SLOT_PAIRS[0])
        w1_second = quantize(w1_grouped[:, SLOT_PAIRS[1]].rearrange("p t n -> p (t n)"), "w1_1")
        w1_first = quantize(w1_grouped[:, SLOT_PAIRS[0]].rearrange("p t n -> p (t n)"), "w1_0")
        w1_mx = (w1_first, w1_second)

        w2_grouped = keep.tile([P, 4, 4 * P], BF16, name="w2_grouped", align_bytes=64)
        for slots in SLOT_PAIRS:
            round_slots("scalar", raw2_low[:], w2_grouped[:, slots, 0 : 2 * P], slots)
        for slots in SLOT_PAIRS:
            round_slots("vector", raw2_high[:], w2_grouped[:, slots, 2 * P : 4 * P], slots)
        w2_mx = [quantize(w2_grouped[:, slots].rearrange("p t n -> p (t n)"), f"w2_{pair}") for pair, slots in enumerate(SLOT_PAIRS)]

        def copy_h(u):
            h_u = shared.tile([P, 2, P // 2, 4], F32, name=f"h_sb{u}", offset=H_PAIR_AT[u // 2] + (u % 2) * H_BYTES)
            entries = slice(u * P, (u + 1) * P)
            bank = multiply(w1_mx, x_code[:, entries], x_scale[:, entries], f"h_bank{u}", u % RING)
            nc.scalar.copy(out=h_u[:], in_=bank[:].rearrange("p t (v d) -> p d v t", d=2))
            return h_u

        def project_e(u):
            entries = slice(u * P, (u + 1) * P)
            return multiply(w2_mx, x_code[:, entries], x_scale[:, entries], f"e_bank{u}", RING + u % RING)

        y_words = keep.tile([P, V], U32, name="y_words", align_bytes=64)
        y_scales = keep.tile([P, V], U8, name="y_scales", align_bytes=64)
        out_rows = out_0.rearrange("(p t) v -> p t v", t=4)
        out_words = out_1[0].rearrange("p c r -> p (c r)").bitcast(I32)

        def pair_sums(q):
            if q == 0:
                z = shared.tile([P, 2, 2 * P], BF16, name="z0", offset=W3_FIRST_AT, align_bytes=64)
            else:
                z = keep.tile([P, 2, 2 * P], BF16, name=f"z{q}", align_bytes=64)
            if q == 1:
                products = shared.tile([P, 2, 2, 2 * P], F32, name="products1", offset=PRODUCTS_1_AT, align_bytes=64)
            else:
                products = keep.tile([P, 2, 2, 2 * P], F32, name=f"products{q}", align_bytes=64)
            for a in range(2):
                u = 2 * q + a
                e_bank = e_first_round[u] if u < RING else project_e(u)
                nc.vector.tensor_tensor(out=products[:, a].rearrange("p d (v t) -> p d v t", t=4),
                                        in0=e_bank[:].rearrange("p t (v d) -> p d v t", d=2),
                                        in1=h_sb[u][:, ::-1], op=ALU.mult)
                if q == QUARTERS - 1:
                    nc.vector.tensor_tensor(out=z[:, a, :], in0=products[:, a, 0, :], in1=products[:, a, 1, :], op=ALU.add)
            if q < QUARTERS - 1:
                adder = nc.gpsimd if q < GPSIMD_ADD_QUARTERS else nc.vector
                adder.tensor_tensor(out=z[:], in0=products[:, :, 0, :], in1=products[:, :, 1, :], op=ALU.add)
            return quantize(z[:].rearrange("p a n -> p (a n)"), f"z{q}")

        h_sb = [copy_h(u) for u in range(RING)]
        e_first_round = [project_e(0), project_e(1)]
        for u in range(RING, RING + 2):
            h_sb.append(copy_h(u))
            e_first_round.append(project_e(u - 2))

        w3_mx = []
        for pair, (engine, at) in enumerate((("gpsimd", W3_FIRST_AT), ("scalar", W3_SECOND_AT))):
            w3_grouped = shared.tile([P, 2, 4 * P], BF16, name=f"w3_grouped{pair}", offset=at, align_bytes=64)
            round_slots(engine, raw3[:], w3_grouped[:], SLOT_PAIRS[pair])
            w3_mx.append(quantize(w3_grouped[:].rearrange("p t n -> p (t n)"), f"w3_{pair}"))
        h_sb.extend(copy_h(u) for u in range(RING + 2, UNITS))
        z_mx = [pair_sums(q) for q in range(QUARTERS)]

        for q in range(QUARTERS):
            records = slice(q * P, (q + 1) * P)
            z_codes, z_scales = z_mx[q]
            bank = multiply(w3_mx, z_codes[:], z_scales[:], f"y_bank{q}", Y_BANK[q])
            y16 = keep.tile([P, 4 * P], BF16, name=f"y16_{q}", align_bytes=64)
            y32 = keep.tile([P, 4, P], F32, name=f"y32_{q}", align_bytes=64)
            nc.scalar.activation(out=y32[:], in_=bank[:], func=ACT.Relu)
            if q < SCALAR_ROUND_QUARTERS:
                nc.scalar.activation(out=y16[:].rearrange("p (v t) -> p v t", t=4), in_=bank[:].rearrange("p t v -> p v t"), func=ACT.Relu)
            else:
                nc.vector.tensor_copy(out=y16[:].rearrange("p (v t) -> p v t", t=4), in_=y32[:].rearrange("p t v -> p v t"))
            nc.vector.quantize_mx(out=y_words[:, records].bitcast(FP8X4), scales=y_scales[:, records], in_=y16[:])
            nc.sync.dma_start(out=out_rows[:, :, records], in_=y32[:])
            if q == QUARTERS - 2:
                nc.sync.dma_start(out=out_words[:, 0 : V - P], in_=y_words[:, 0 : V - P].bitcast(I32))
        nc.sync.dma_start(out=out_words[:, V - P : V], in_=y_words[:, V - P : V].bitcast(I32))
        for quadrant in range(4):
            queue = nc.sync if quadrant % 2 == 0 else nc.scalar
            queue.dma_start(out=out_2[0, 4 * quadrant : 4 * quadrant + 4, :].bitcast(I32),
                            in_=y_scales[32 * quadrant : 32 * quadrant + 4, :].bitcast(I32))
